import numpy as np
import ml_dtypes


def mxq(x, axis, fmt="e4m3"):
    dtype, down = {"e4m3": (ml_dtypes.float8_e4m3fn, 7), "e5m2": (ml_dtypes.float8_e5m2, 14)}[fmt]
    v = np.moveaxis(np.asarray(x, np.float32).astype(ml_dtypes.bfloat16).astype(np.float64), axis, -1)
    blocks = v.reshape(v.shape[:-1] + (-1, 32))
    amax = np.abs(blocks).max(-1, keepdims=True)
    byte = np.maximum(np.where(amax > 0, np.frexp(amax)[1] - 1 + 127, 0) - down, 1)
    scale = np.exp2(byte - 127.0)
    codes = (blocks / scale).astype(np.float32).astype(dtype).astype(np.float64)
    return np.moveaxis((codes * scale).reshape(v.shape), -1, axis)


WIDE = False


def mx_kscale(k):
    if not WIDE:
        return np.ones(k)
    levels = np.array([10, -10, 5, -5, 0])
    if k % 512:
        return np.exp2(np.random.permutation(np.resize(levels, k // 32))).repeat(32)
    a = np.empty((k // 512, 16))
    for p in range(k // 512):
        a[p, :8] = np.random.permutation(np.resize(levels, 8))
        for g in range(8):
            far = levels[np.abs(levels - a[p, g]) >= 10]
            a[p, g + 8] = far[np.random.randint(len(far))]
    return np.exp2(a.ravel()).repeat(32)


def f64(x):
    return np.asarray(x).astype(np.float64)


def striped(idx):
    return np.tile(idx.reshape(-1, 16).T, (8, 1)).astype(np.uint16)


def unstriped(offs):
    return offs[:16].T.reshape(-1).astype(np.int64)


K, T, D, S, V, R, N = 1024, 1024, 4, 512, 128, 8, 512


def setup_inputs():
    n = np.random.standard_normal
    s = mx_kscale(K)[:, None]
    return {
        "xT": (n((K, T)) * s).astype(np.float32),
        "w": (n((D, K, N)) / np.sqrt(D * K) / s[None]).astype(np.float32),
        "offs": striped(np.concatenate([R * np.arange(V) + np.random.randint(0, R, V) for _ in range(D)])),
    }


def reference(xT, w, offs):
    idx = unstriped(offs)
    xq = mxq(f64(xT)[:, idx], 0, "e4m3")
    wq = mxq(f64(w), 1, "e4m3")
    y = sum(wq[d].T @ xq[:, d * V:(d + 1) * V] for d in range(D))
    return y

@@ -1,0 +1,144 @@
+import concourse.mybir as mybir
+
+D, K, T, S, V, M = 4, 1024, 1024, 512, 128, 512
+FLOPS = 2 * K * M * S
+
+F32 = mybir.dt.float32
+BF16 = mybir.dt.bfloat16
+U32 = mybir.dt.uint32
+U16 = mybir.dt.uint16
+U8 = mybir.dt.uint8
+FP8X4 = mybir.dt.float8_e4m3fn_x4
+
+P = 128
+PACK = 4
+K_PASS = P * PACK
+PASSES = K // K_PASS
+M_TILE = 128
+ALIGN = 64
+
+LOAD_ORDER = (
+    ("w", 0, 0), ("w", 1, 0), ("x", 0), ("w", 2, 0), ("w", 3, 0), ("x", 1), ("w", 0, 1), ("w", 1, 1), ("w", 2, 1), ("w", 3, 1),
+)
+LAST = LOAD_ORDER[-1]
+LAST_PIECES = ((0, 256, 96), (256, 128, 48), (384, 128, 48))
+X_HALF = T // 2
+X_SCALAR = 320
+W_SCALAR = 288
+
+
+def interleave(nc, grouped, raw, raw0, g0, width, scalar_columns):
+    def views(lo, hi):
+        dst = grouped[:, g0 + lo : g0 + hi, :].rearrange("p (c i) j -> p c j i", i=4)
+        src = raw[:, :, raw0 + lo : raw0 + hi].rearrange("p j (c i) -> p c j i", i=4)
+        return dst, src
+
+    dst, src = views(0, scalar_columns)
+    nc.scalar.copy(out=dst, in_=src)
+    dst, src = views(scalar_columns, width)
+    nc.vector.tensor_copy(out=dst, in_=src)
+
+
+def tile_picked_deform_lin_none_def_e_kernel(tc, xT, w, offs, out):
+    nc = tc.nc
+    with tc.tile_pool(name="keep", bufs=1) as keep, tc.psum_pool(name="psum", bufs=1) as psum:
+        offsets = keep.tile([P, S // 16], U16, name="offsets")
+
+        warm = keep.tile([P, 1], F32, name="warm")
+        warm_out = keep.tile([P, 1], F32, name="warm_out")
+        nc.vector.memset(warm[:], 0.0)
+        nc.scalar.copy(out=warm_out[:], in_=warm[:])
+
+        x_raw, x_grouped, x_codes, x_scales, g_codes, g_scales = [], [], [], [], [], []
+        for a in range(PASSES):
+            x_raw.append(keep.tile([P, PACK, T], F32, name=f"x_raw{a}"))
+            x_grouped.append(keep.tile([P, T, PACK], BF16, name=f"x_grouped{a}", align_bytes=ALIGN))
+            x_codes.append(keep.tile([P, T], U32, name=f"x_codes{a}", align_bytes=ALIGN))
+            x_scales.append(keep.tile([P, T], U8, name=f"x_scales{a}", align_bytes=ALIGN))
+            g_codes.append(keep.tile([P, S], U32, name=f"g_codes{a}", align_bytes=ALIGN))
+            g_scales.append(keep.tile([P, S], U8, name=f"g_scales{a}", align_bytes=ALIGN))
+            nc.gpsimd.memset(x_scales[a][:], 0)
+
+        blocks = []
+        for i, item in enumerate(LOAD_ORDER):
+            if item[0] == "x":
+                a = item[1]
+                nc.sync.dma_start(out=x_raw[a][:], in_=xT[a * K_PASS : (a + 1) * K_PASS, :].rearrange("(p j) t -> p j t", j=PACK))
+                for c0 in range(0, T, X_HALF):
+                    blocks.append(("x", a, c0))
+            else:
+                d, a = item[1], item[2]
+                rows = w[d, a * K_PASS : (a + 1) * K_PASS, :].rearrange("(p j) m -> p j m", j=PACK)
+                pieces = LAST_PIECES if item == LAST else ((0, M, W_SCALAR),)
+                for c0, width, scalar_columns in pieces:
+                    tag = f"{d}_{a}_{c0}"
+                    raw = keep.tile([P, PACK, width], F32, name=f"w_raw{tag}")
+                    nc.sync.dma_start(out=raw[:], in_=rows[:, :, c0 : c0 + width])
+                    grouped = keep.tile([P, width, PACK], BF16, name=f"w_grouped{tag}", align_bytes=ALIGN)
+                    codes = keep.tile([P, width], U32, name=f"w_codes{tag}", align_bytes=ALIGN)
+                    scales = keep.tile([P, width], U8, name=f"w_scales{tag}", align_bytes=ALIGN)
+                    blocks.append(("w", d, a, c0, width, scalar_columns, raw, grouped, codes, scales))
+            if i == 1:
+                nc.sync.dma_start(offsets[:], offs)
+
+        acc = [psum.tile([M_TILE, V], F32, name=f"acc{m}") for m in range(M // M_TILE)]
+        done = [0] * len(acc)
+        gathered = [False] * PASSES
+        waiting = []
+
+        def copy(block):
+            if block[0] == "x":
+                a, c0 = block[1], block[2]
+                interleave(nc, x_grouped[a], x_raw[a], c0, c0, X_HALF, X_SCALAR)
+            else:
+                width, scalar_columns, raw, grouped = block[4], block[5], block[6], block[7]
+                interleave(nc, grouped, raw, 0, 0, width, scalar_columns)
+
+        def multiply(block):
+            d, a, c0, width, codes, scales = block[1], block[2], block[3], block[4], block[8], block[9]
+            for lo in range(0, width, M_TILE):
+                m = (c0 + lo) // M_TILE
+                nc.tensor.matmul_mx(
+                    out=acc[m][:],
+                    lhsT=codes[:, lo : lo + M_TILE].bitcast(FP8X4),
+                    lhsT_scale=scales[:, lo : lo + M_TILE],
+                    rhs=g_codes[a][:, d * V : (d + 1) * V].bitcast(FP8X4),
+                    rhs_scale=g_scales[a][:, d * V : (d + 1) * V],
+                    start=(done[m] == 0),
+                    stop=(done[m] == D * PASSES - 1),
+                )
+                done[m] += 1
+                if done[m] == D * PASSES:
+                    result = keep.tile([M_TILE, V], F32, name=f"result{m}")
+                    nc.scalar.copy(out=result[:], in_=acc[m][:])
+                    nc.sync.dma_start(out=out[m * M_TILE : (m + 1) * M_TILE, :], in_=result[:])
+
+        def quantize(block):
+            if block[0] == "x":
+                a, c0 = block[1], block[2]
+                cols = slice(c0, c0 + X_HALF)
+                nc.vector.quantize_mx(
+                    out=x_codes[a][:, cols].bitcast(FP8X4),
+                    scales=x_scales[a][:, cols],
+                    in_=x_grouped[a][:, cols, :].rearrange("p c j -> p (c j)"),
+                )
+                if c0 + X_HALF == T:
+                    nc.vector.tensor_copy(g_codes[a][:], x_codes[a][:].indirect(offsets[:]))
+                    nc.vector.tensor_copy(g_scales[a][:], x_scales[a][:].indirect(offsets[:]))
+                    gathered[a] = True
+            else:
+                nc.vector.quantize_mx(
+                    out=block[8][:].bitcast(FP8X4),
+                    scales=block[9][:],
+                    in_=block[7][:].rearrange("p c j -> p (c j)"),
+                )
+                waiting.append(block)
+            for ready in [b for b in waiting if gathered[b[2]]]:
+                waiting.remove(ready)
+                multiply(ready)
+
+        for step in range(len(blocks) + 1):
+            if step < len(blocks):
+                copy(blocks[step])
+            if step > 0:
+                quantize(blocks[step - 1])

@@ -17,25 +17,26 @@ PASSES = K // K_PASS
 M_TILE = 128
 ALIGN = 64
 
-LOAD_ORDER = (
-    ("w", 0, 0), ("w", 1, 0), ("x", 0), ("w", 2, 0), ("w", 3, 0), ("x", 1), ("w", 0, 1), ("w", 1, 1), ("w", 2, 1), ("w", 3, 1),
+LOADS = (
+    ("x", 0), ("w", 0), ("x", 1), ("w", 1), ("w", 2), ("w", 3, 0, 0, M), ("w", 3, 1, 0, 256), ("w", 3, 1, 256, 128), ("w", 3, 1, 384, 128),
 )
-LAST = LOAD_ORDER[-1]
-LAST_PIECES = ((0, 256, 96), (256, 128, 48), (384, 128, 48))
 X_HALF = T // 2
 X_SCALAR = 320
-W_SCALAR = 288
 
 
-def interleave(nc, grouped, raw, raw0, g0, width, scalar_columns):
-    def views(lo, hi):
-        dst = grouped[:, g0 + lo : g0 + hi, :].rearrange("p (c i) j -> p c j i", i=4)
-        src = raw[:, :, raw0 + lo : raw0 + hi].rearrange("p j (c i) -> p c j i", i=4)
+def w_scalar(width):
+    return 288 * width // M if width == M else 96 * width // 256
+
+
+def interleave(nc, grouped, raw, scalar_columns):
+    def views(cols):
+        dst = grouped[:, cols, :].rearrange("p (c i) j -> p c j i", i=4)
+        src = raw[:, :, cols].rearrange("p j (c i) -> p c j i", i=4)
         return dst, src
 
-    dst, src = views(0, scalar_columns)
+    dst, src = views(slice(0, scalar_columns))
     nc.scalar.copy(out=dst, in_=src)
-    dst, src = views(scalar_columns, width)
+    dst, src = views(slice(scalar_columns, raw.shape[2]))
     nc.vector.tensor_copy(out=dst, in_=src)
 
 
@@ -60,25 +61,34 @@ def tile_picked_deform_lin_none_def_e_kernel(tc, xT, w, offs, out):
             nc.gpsimd.memset(x_scales[a][:], 0)
 
         blocks = []
-        for i, item in enumerate(LOAD_ORDER):
+
+        def add_w(d, a, c0, raw):
+            width = raw.shape[2]
+            tag = f"{d}_{a}_{c0}"
+            grouped = keep.tile([P, width, PACK], BF16, name=f"w_grouped{tag}", align_bytes=ALIGN)
+            codes = keep.tile([P, width], U32, name=f"w_codes{tag}", align_bytes=ALIGN)
+            scales = keep.tile([P, width], U8, name=f"w_scales{tag}", align_bytes=ALIGN)
+            blocks.append(("w", d, a, c0, raw, grouped, codes, scales))
+
+        for i, item in enumerate(LOADS):
             if item[0] == "x":
                 a = item[1]
                 nc.sync.dma_start(out=x_raw[a][:], in_=xT[a * K_PASS : (a + 1) * K_PASS, :].rearrange("(p j) t -> p j t", j=PACK))
                 for c0 in range(0, T, X_HALF):
                     blocks.append(("x", a, c0))
+            elif len(item) == 2:
+                d = item[1]
+                raw = keep.tile([P, PASSES, PACK, M], F32, name=f"w_raw{d}")
+                nc.sync.dma_start(out=raw[:], in_=w[d].rearrange("(a p j) m -> p a j m", a=PASSES, j=PACK))
+                for a in range(PASSES):
+                    add_w(d, a, 0, raw[:, a, :, :])
             else:
-                d, a = item[1], item[2]
+                d, a, c0, width = item[1:]
                 rows = w[d, a * K_PASS : (a + 1) * K_PASS, :].rearrange("(p j) m -> p j m", j=PACK)
-                pieces = LAST_PIECES if item == LAST else ((0, M, W_SCALAR),)
-                for c0, width, scalar_columns in pieces:
-                    tag = f"{d}_{a}_{c0}"
-                    raw = keep.tile([P, PACK, width], F32, name=f"w_raw{tag}")
-                    nc.sync.dma_start(out=raw[:], in_=rows[:, :, c0 : c0 + width])
-                    grouped = keep.tile([P, width, PACK], BF16, name=f"w_grouped{tag}", align_bytes=ALIGN)
-                    codes = keep.tile([P, width], U32, name=f"w_codes{tag}", align_bytes=ALIGN)
-                    scales = keep.tile([P, width], U8, name=f"w_scales{tag}", align_bytes=ALIGN)
-                    blocks.append(("w", d, a, c0, width, scalar_columns, raw, grouped, codes, scales))
-            if i == 1:
+                raw = keep.tile([P, PACK, width], F32, name=f"w_raw{d}_{a}_{c0}")
+                nc.sync.dma_start(out=raw[:], in_=rows[:, :, c0 : c0 + width])
+                add_w(d, a, c0, raw[:])
+            if i == 0:
                 nc.sync.dma_start(offsets[:], offs)
 
         acc = [psum.tile([M_TILE, V], F32, name=f"acc{m}") for m in range(M // M_TILE)]
@@ -89,14 +99,15 @@ def tile_picked_deform_lin_none_def_e_kernel(tc, xT, w, offs, out):
         def copy(block):
             if block[0] == "x":
                 a, c0 = block[1], block[2]
-                interleave(nc, x_grouped[a], x_raw[a], c0, c0, X_HALF, X_SCALAR)
+                cols = slice(c0, c0 + X_HALF)
+                interleave(nc, x_grouped[a][:, cols, :], x_raw[a][:, :, cols], X_SCALAR)
             else:
-                width, scalar_columns, raw, grouped = block[4], block[5], block[6], block[7]
-                interleave(nc, grouped, raw, 0, 0, width, scalar_columns)
+                raw, grouped = block[4], block[5]
+                interleave(nc, grouped[:], raw, w_scalar(raw.shape[2]))
 
         def multiply(block):
-            d, a, c0, width, codes, scales = block[1], block[2], block[3], block[4], block[8], block[9]
-            for lo in range(0, width, M_TILE):
+            d, a, c0, raw, grouped, codes, scales = block[1:]
+            for lo in range(0, raw.shape[2], M_TILE):
                 m = (c0 + lo) // M_TILE
                 nc.tensor.matmul_mx(
                     out=acc[m][:],
@@ -128,9 +139,9 @@ def tile_picked_deform_lin_none_def_e_kernel(tc, xT, w, offs, out):
                     gathered[a] = True
             else:
                 nc.vector.quantize_mx(
-                    out=block[8][:].bitcast(FP8X4),
-                    scales=block[9][:],
-                    in_=block[7][:].rearrange("p c j -> p (c j)"),
+                    out=block[6][:].bitcast(FP8X4),
+                    scales=block[7][:],
+                    in_=block[5][:].rearrange("p c j -> p (c j)"),
                 )
                 waiting.append(block)
             for ready in [b for b in waiting if gathered[b[2]]]:

@@ -30,8 +30,8 @@ def w_scalar(width):
 
 def interleave(nc, grouped, raw, scalar_columns):
     def views(cols):
-        dst = grouped[:, cols, :].rearrange("p (c i) j -> p c j i", i=4)
-        src = raw[:, :, cols].rearrange("p j (c i) -> p c j i", i=4)
+        dst = grouped[:, cols, :].rearrange("p (c i) j -> p c j i", i=2)
+        src = raw[:, :, cols].rearrange("p j (c i) -> p c j i", i=2)
         return dst, src
 
     dst, src = views(slice(0, scalar_columns))

import concourse.mybir as mybir

D, K, T, S, V, M = 4, 1024, 1024, 512, 128, 512
FLOPS = 2 * K * M * S

F32 = mybir.dt.float32
BF16 = mybir.dt.bfloat16
U32 = mybir.dt.uint32
U16 = mybir.dt.uint16
U8 = mybir.dt.uint8
FP8X4 = mybir.dt.float8_e4m3fn_x4

P = 128
PACK = 4
K_PASS = P * PACK
PASSES = K // K_PASS
M_TILE = 128
ALIGN = 64

LOADS = (
    ("x", 0), ("w", 0), ("x", 1), ("w", 1), ("w", 2), ("w", 3, 0, 0, M), ("w", 3, 1, 0, 256), ("w", 3, 1, 256, 128), ("w", 3, 1, 384, 128),
)
X_HALF = T // 2
X_SCALAR = 320


def w_scalar(width):
    return 288 * width // M if width == M else 96 * width // 256


def interleave(nc, grouped, raw, scalar_columns):
    def views(cols):
        dst = grouped[:, cols, :].rearrange("p (c i) j -> p c j i", i=2)
        src = raw[:, :, cols].rearrange("p j (c i) -> p c j i", i=2)
        return dst, src

    dst, src = views(slice(0, scalar_columns))
    nc.scalar.copy(out=dst, in_=src)
    dst, src = views(slice(scalar_columns, raw.shape[2]))
    nc.vector.tensor_copy(out=dst, in_=src)


def tile_picked_deform_lin_none_def_e_kernel(tc, xT, w, offs, out):
    nc = tc.nc
    with tc.tile_pool(name="keep", bufs=1) as keep, tc.psum_pool(name="psum", bufs=1) as psum:
        offsets = keep.tile([P, S // 16], U16, name="offsets")

        warm = keep.tile([P, 1], F32, name="warm")
        warm_out = keep.tile([P, 1], F32, name="warm_out")
        nc.vector.memset(warm[:], 0.0)
        nc.scalar.copy(out=warm_out[:], in_=warm[:])

        x_raw, x_grouped, x_codes, x_scales, g_codes, g_scales = [], [], [], [], [], []
        for a in range(PASSES):
            x_raw.append(keep.tile([P, PACK, T], F32, name=f"x_raw{a}"))
            x_grouped.append(keep.tile([P, T, PACK], BF16, name=f"x_grouped{a}", align_bytes=ALIGN))
            x_codes.append(keep.tile([P, T], U32, name=f"x_codes{a}", align_bytes=ALIGN))
            x_scales.append(keep.tile([P, T], U8, name=f"x_scales{a}", align_bytes=ALIGN))
            g_codes.append(keep.tile([P, S], U32, name=f"g_codes{a}", align_bytes=ALIGN))
            g_scales.append(keep.tile([P, S], U8, name=f"g_scales{a}", align_bytes=ALIGN))
            nc.gpsimd.memset(x_scales[a][:], 0)

        blocks = []

        def add_w(d, a, c0, raw):
            width = raw.shape[2]
            tag = f"{d}_{a}_{c0}"
            grouped = keep.tile([P, width, PACK], BF16, name=f"w_grouped{tag}", align_bytes=ALIGN)
            codes = keep.tile([P, width], U32, name=f"w_codes{tag}", align_bytes=ALIGN)
            scales = keep.tile([P, width], U8, name=f"w_scales{tag}", align_bytes=ALIGN)
            blocks.append(("w", d, a, c0, raw, grouped, codes, scales))

        for i, item in enumerate(LOADS):
            if item[0] == "x":
                a = item[1]
                nc.sync.dma_start(out=x_raw[a][:], in_=xT[a * K_PASS : (a + 1) * K_PASS, :].rearrange("(p j) t -> p j t", j=PACK))
                for c0 in range(0, T, X_HALF):
                    blocks.append(("x", a, c0))
            elif len(item) == 2:
                d = item[1]
                raw = keep.tile([P, PASSES, PACK, M], F32, name=f"w_raw{d}")
                nc.sync.dma_start(out=raw[:], in_=w[d].rearrange("(a p j) m -> p a j m", a=PASSES, j=PACK))
                for a in range(PASSES):
                    add_w(d, a, 0, raw[:, a, :, :])
            else:
                d, a, c0, width = item[1:]
                rows = w[d, a * K_PASS : (a + 1) * K_PASS, :].rearrange("(p j) m -> p j m", j=PACK)
                raw = keep.tile([P, PACK, width], F32, name=f"w_raw{d}_{a}_{c0}")
                nc.sync.dma_start(out=raw[:], in_=rows[:, :, c0 : c0 + width])
                add_w(d, a, c0, raw[:])
            if i == 0:
                nc.sync.dma_start(offsets[:], offs)

        acc = [psum.tile([M_TILE, V], F32, name=f"acc{m}") for m in range(M // M_TILE)]
        done = [0] * len(acc)
        gathered = [False] * PASSES
        waiting = []

        def copy(block):
            if block[0] == "x":
                a, c0 = block[1], block[2]
                cols = slice(c0, c0 + X_HALF)
                interleave(nc, x_grouped[a][:, cols, :], x_raw[a][:, :, cols], X_SCALAR)
            else:
                raw, grouped = block[4], block[5]
                interleave(nc, grouped[:], raw, w_scalar(raw.shape[2]))

        def multiply(block):
            d, a, c0, raw, grouped, codes, scales = block[1:]
            for lo in range(0, raw.shape[2], M_TILE):
                m = (c0 + lo) // M_TILE
                nc.tensor.matmul_mx(
                    out=acc[m][:],
                    lhsT=codes[:, lo : lo + M_TILE].bitcast(FP8X4),
                    lhsT_scale=scales[:, lo : lo + M_TILE],
                    rhs=g_codes[a][:, d * V : (d + 1) * V].bitcast(FP8X4),
                    rhs_scale=g_scales[a][:, d * V : (d + 1) * V],
                    start=(done[m] == 0),
                    stop=(done[m] == D * PASSES - 1),
                )
                done[m] += 1
                if done[m] == D * PASSES:
                    result = keep.tile([M_TILE, V], F32, name=f"result{m}")
                    nc.scalar.copy(out=result[:], in_=acc[m][:])
                    nc.sync.dma_start(out=out[m * M_TILE : (m + 1) * M_TILE, :], in_=result[:])

        def quantize(block):
            if block[0] == "x":
                a, c0 = block[1], block[2]
                cols = slice(c0, c0 + X_HALF)
                nc.vector.quantize_mx(
                    out=x_codes[a][:, cols].bitcast(FP8X4),
                    scales=x_scales[a][:, cols],
                    in_=x_grouped[a][:, cols, :].rearrange("p c j -> p (c j)"),
                )
                if c0 + X_HALF == T:
                    nc.vector.tensor_copy(g_codes[a][:], x_codes[a][:].indirect(offsets[:]))
                    nc.vector.tensor_copy(g_scales[a][:], x_scales[a][:].indirect(offsets[:]))
                    gathered[a] = True
            else:
                nc.vector.quantize_mx(
                    out=block[6][:].bitcast(FP8X4),
                    scales=block[7][:],
                    in_=block[5][:].rearrange("p c j -> p (c j)"),
                )
                waiting.append(block)
            for ready in [b for b in waiting if gathered[b[2]]]:
                waiting.remove(ready)
                multiply(ready)

        for step in range(len(blocks) + 1):
            if step < len(blocks):
                copy(blocks[step])
            if step > 0:
                quantize(blocks[step - 1])
